import numpy as np
import ml_dtypes


def mxq(x, axis, fmt="e4m3"):
    dtype, down = {"e4m3": (ml_dtypes.float8_e4m3fn, 7), "e5m2": (ml_dtypes.float8_e5m2, 14)}[fmt]
    v = np.moveaxis(np.asarray(x, np.float32).astype(ml_dtypes.bfloat16).astype(np.float64), axis, -1)
    blocks = v.reshape(v.shape[:-1] + (-1, 32))
    amax = np.abs(blocks).max(-1, keepdims=True)
    byte = np.maximum(np.where(amax > 0, np.frexp(amax)[1] - 1 + 127, 0) - down, 1)
    scale = np.exp2(byte - 127.0)
    codes = (blocks / scale).astype(np.float32).astype(dtype).astype(np.float64)
    return np.moveaxis((codes * scale).reshape(v.shape), -1, axis)


WIDE = False


def mx_kscale(k):
    if not WIDE:
        return np.ones(k)
    levels = np.array([10, -10, 5, -5, 0])
    if k % 512:
        return np.exp2(np.random.permutation(np.resize(levels, k // 32))).repeat(32)
    a = np.empty((k // 512, 16))
    for p in range(k // 512):
        a[p, :8] = np.random.permutation(np.resize(levels, 8))
        for g in range(8):
            far = levels[np.abs(levels - a[p, g]) >= 10]
            a[p, g + 8] = far[np.random.randint(len(far))]
    return np.exp2(a.ravel()).repeat(32)


BF16 = ml_dtypes.bfloat16


def bf(x):
    return np.asarray(x, np.float32).astype(BF16)


def f64(x):
    return np.asarray(x).astype(np.float64)


E2M1 = np.array([0.0, 0.5, 1.0, 1.5, 2.0, 3.0, 4.0, 6.0, -0.0, -0.5, -1.0, -1.5, -2.0, -3.0, -4.0, -6.0])


def pack_weight(w, fmt):
    k, n = w.shape
    w = f64(bf(w)).reshape(k // 32, 32, n)
    amax = np.abs(w).max(1)
    if fmt == "e4m3":
        byte = np.frexp(amax)[1] - 1 + 127 - 7
    else:
        mant, ex = np.frexp(amax / 6.0)
        byte = np.where(mant > 0.5, ex, ex - 1) + 127
    byte = np.clip(np.where(amax > 0, byte, 1), 1, 254)
    scaled = (w * np.exp2(127.0 - byte)[:, None, :]).reshape(k, n).astype(np.float32)
    by_word = np.ascontiguousarray(scaled.reshape(k // 512, 128, 4, n).transpose(0, 1, 3, 2))
    if fmt == "e4m3":
        words = by_word.astype(ml_dtypes.float8_e4m3fn).view(np.uint8)
    else:
        c = by_word.astype(ml_dtypes.float4_e2m1fn).view(np.uint8) & 0xF
        words = c[..., 0::2] | (c[..., 1::2] << 4)
    return np.ascontiguousarray(words), np.ascontiguousarray(byte.astype(np.uint8).reshape(k // 512, 16, n))


def unpack_weight(words, scales, fmt):
    g, p, n, _ = words.shape
    if fmt == "e4m3":
        vals = np.ascontiguousarray(words).view(ml_dtypes.float8_e4m3fn).astype(np.float64)
    else:
        nib = np.empty((g, p, n, 4), np.uint8)
        nib[..., 0::2] = words & 0xF
        nib[..., 1::2] = words >> 4
        vals = E2M1[nib]
    vals = vals * np.repeat(np.exp2(scales.astype(np.float64) - 127.0), 8, axis=1)[..., None]
    return vals.transpose(0, 1, 3, 2).reshape(g * 512, n)
def pack4(w):
    words, scales = pack_weight(w, "e2m1")
    return words.reshape(words.shape[0], 128, -1), scales


def unpack4(words, scales):
    return unpack_weight(words.reshape(words.shape[0], 128, -1, 2), scales, "e2m1")


G, M, T, A, N = 4, 512, 1024, 512, 512


def setup_inputs():
    s, t = mx_kscale(G * T), mx_kscale(G * A)
    alpha = np.random.uniform(0.05, 0.45, (G, 1, A))
    phase = 2 * np.pi * alpha * np.arange(T)[None, :, None]
    basis = np.concatenate([np.cos(phase), np.sin(phase)], axis=2) * np.sqrt(2 / T)
    basis_words, basis_scales = pack4(basis.reshape(G * T, 2 * A) / s[:, None])
    sig = np.random.standard_normal((G * A, N)) / np.sqrt(A)
    sig_words, sig_scales = pack4(sig / t[:, None])
    return {"x": bf(np.random.standard_normal((G, M, T)) * s.reshape(G, 1, T)),
            "basis_words": basis_words,
            "basis_scales": basis_scales,
            "v": bf((1 + 0.1 * np.random.standard_normal((G, A))) * t.reshape(G, A)),
            "sig_words": sig_words,
            "sig_scales": sig_scales}


def reference(x, basis_words, basis_scales, v, sig_words, sig_scales):
    basis = unpack4(basis_words, basis_scales).reshape(G, T, 2 * A)
    sig = unpack4(sig_words, sig_scales).reshape(G, A, N)
    z = mxq(f64(x), 2, "e4m3") @ basis
    power = np.square(z).reshape(G, M, 2, A).sum(axis=2)
    e = power * f64(v)[:, None, :]
    return mxq(e, 2, "e4m3") @ sig

@@ -1,0 +1,537 @@
+from contextlib import ExitStack
+
+import concourse.mybir as mybir
+from concourse.masks import make_identity
+
+G, M, T, A, N = 4, 512, 1024, 512, 512
+FLOPS = G * (2 * M * T * 2 * A + 2 * M * A * N)
+
+F32 = mybir.dt.float32
+BF16 = mybir.dt.bfloat16
+U32 = mybir.dt.uint32
+I32 = mybir.dt.int32
+U8 = mybir.dt.uint8
+FP8X4 = mybir.dt.float8_e4m3fn_x4
+FP4X4 = mybir.dt.float4_e2m1fn_x4
+ACT = mybir.ActivationFunctionType
+ALU = mybir.AluOpType
+
+P = 128
+PAIRS = G * M // 256
+Z_BANKS = 3
+O_BANKS = 2
+
+
+def tile_cyclostationary_band_detector_s14_kernel(tc, x, basis_words, basis_scales, v, sig_words, sig_scales, out):
+    nc = tc.nc
+    with ExitStack() as ctx:
+        keep = ctx.enter_context(tc.tile_pool(name="keep", bufs=1))
+        work = ctx.enter_context(tc.tile_pool(name="work", bufs=6))
+        psum = ctx.enter_context(tc.psum_pool(name="psum", bufs=1))
+        ctx.enter_context(tc.manual_schedule())
+
+        dummy = keep.tile([P, 16], F32, name="dummy")
+        nc.vector.memset(dummy[:], 0.0)
+        plane0 = keep.tile([P, 2 * 2 * A], U8, name="plane0", align_bytes=64)
+        plane1 = keep.tile([P, 3 * 2 * 2 * A], U8, name="plane1", align_bytes=64)
+        splane = keep.tile([P, G * N], U8, name="splane", align_bytes=64)
+        vrow = keep.tile([P, G * A], BF16, name="vrow")
+        ones = keep.tile([P, P], BF16, name="ones")
+        ident = keep.tile([P, P], F32, name="ident")
+        vb = keep.tile([P, G * A], BF16, name="vb")
+        vcol = keep.tile([P, 4], BF16, name="vcol")
+        nc.vector.memset(vrow[:].bitcast(I32), 0)
+        nc.vector.memset(plane0[:].bitcast(I32), 0)
+        make_identity(nc, ident[:])
+        nc.gpsimd.memset(ones[:], 1.0)
+        nc.vector.memset(splane[:].bitcast(I32), 0)
+        nc.vector.memset(plane1[:].bitcast(I32), 0)
+        nc.scalar.activation(out=dummy[:], in_=dummy[:], func=ACT.Square)
+
+        x_sb = [keep.tile([P, 2, T], BF16, name="x%d" % j) for j in range(PAIRS)]
+        bw = [keep.tile([P, 2, 4 * A], U8, name="bw%d" % b, align_bytes=64) for b in range(G)]
+        sw = keep.tile([P, G, 2 * N], U8, name="sw", align_bytes=64)
+
+        def load_x(j, h):
+            r0 = (j % 2) * 256 + h * 128
+            nc.sync.dma_start(out=x_sb[j][:, h, :], in_=x[j // 2, r0 : r0 + 128, :])
+
+        def load_x_pair(j):
+            r0 = (j % 2) * 256
+            nc.sync.dma_start(out=x_sb[j][:], in_=x[j // 2, r0 : r0 + 256, :].rearrange("(h p) k -> p h k", p=P))
+
+        def load_scales(tile, src, r, eng):
+            eng.dma_start(
+                out=tile[r:P:32, :].bitcast(I32).rearrange("q (g n) -> q g n", g=src.shape[0]),
+                in_=src[:, r:16:4, :].bitcast(I32).rearrange("g q n -> q g n"),
+            )
+
+        nc.scalar.dma_start(out=vrow[0:1, :], in_=v.rearrange("(o b) a -> o (b a)", o=1))
+        load_x(0, 0)
+        load_x(0, 1)
+        for r in range(4):
+            load_scales(plane0, basis_scales[0:2], r, nc.scalar if r < 2 else nc.gpsimd)
+        load_x_pair(1)
+        for g in range(2):
+            nc.sync.dma_start(out=bw[0][:, g, :], in_=basis_words[g])
+        load_x_pair(2)
+        for r in range(4):
+            load_scales(plane1, basis_scales[2:8], r, nc.gpsimd)
+        for r in range(4):
+            load_scales(splane, sig_scales, r, nc.gpsimd)
+        for b in range(1, G):
+            nc.sync.dma_start(out=bw[b][:], in_=basis_words[2 * b : 2 * b + 2].rearrange("g p n -> p g n"))
+            load_x_pair(2 * b + 1)
+            if b == 1:
+                nc.sync.dma_start(out=sw[:], in_=sig_words.rearrange("b p n -> p b n"))
+            if b + 1 < G:
+                load_x_pair(2 * b + 2)
+        nc.sync.dma_start(out=vcol[:], in_=v[G - 1].rearrange("(p t) -> p t", t=4))
+
+        def basis_plane(b):
+            return plane0[:] if b == 0 else plane1[:, 2048 * (b - 1) : 2048 * b]
+
+        z_count = [0]
+        o_count = [0]
+
+        def bank(name):
+            return psum.tile([P, 512], F32, name=name)
+
+        def z_bank():
+            z_count[0] += 1
+            return bank("z%d" % (z_count[0] % Z_BANKS))
+
+        def o_name():
+            o_count[0] += 1
+            return "o%d" % (o_count[0] % O_BANKS)
+
+        def o_bank():
+            return bank(o_name())
+
+        vbank = {}
+
+        xt, xg, xc, xs = {}, {}, {}, {}
+        zb, sq, pw, e = {}, {}, {}, {}
+        et, eg, ec, es = {}, {}, {}, {}
+        ob, osb = {}, {}
+
+        def t_x(j, h):
+            t = bank("xt%d" % h)
+            xt[j, h] = t
+            words = x_sb[j][:, h, :].bitcast(F32)
+            for g in range(2):
+                for u in range(2):
+                    c = (2 * g + u) * P
+                    nc.tensor.transpose(t[:, c : c + P], words[:, 256 * g + u : 256 * (g + 1) : 2], ident[:])
+
+        def copy_x(j, h, eng):
+            if j not in xg:
+                xg[j] = work.tile([P, 2048], BF16, name="xg", align_bytes=64)
+            dst = xg[j][:, 1024 * h : 1024 * (h + 1)].bitcast(F32).rearrange("p (g r u) -> p g r u", g=2, u=2)
+            src = xt[j, h][:].rearrange("p (g u r) -> p g r u", g=2, u=2)
+            if eng is nc.scalar:
+                nc.scalar.copy(out=dst, in_=src)
+            else:
+                nc.vector.tensor_copy(out=dst, in_=src)
+
+        def q_x(j, h0, h1):
+            if j not in xc:
+                xc[j] = work.tile([P, 512], U32, name="xc", align_bytes=64)
+                xs[j] = work.tile([P, 512], U8, name="xs", align_bytes=64)
+            nc.vector.quantize_mx(
+                out=xc[j][:, 256 * h0 : 256 * h1].bitcast(FP8X4),
+                scales=xs[j][:, 256 * h0 : 256 * h1],
+                in_=xg[j][:, 1024 * h0 : 1024 * h1],
+            )
+
+        def m1(j, h, s):
+            b = j // 2
+            t = z_bank()
+            zb[j, h, s] = t
+            for g in range(2):
+                c = (2 * h + g) * P
+                nc.tensor.matmul_mx(
+                    out=t[:],
+                    lhsT=xc[j][:, c : c + P].bitcast(FP8X4),
+                    lhsT_scale=xs[j][:, c : c + P],
+                    rhs=bw[b][:, g, 1024 * s : 1024 * (s + 1)].bitcast(FP4X4),
+                    rhs_scale=basis_plane(b)[:, 1024 * g + 512 * s : 1024 * g + 512 * (s + 1)],
+                    start=(g == 0),
+                    stop=(g == 1),
+                )
+
+        def square_part(j, h, s, half):
+            if half == 0:
+                sq[j, h, s] = work.tile([P, 512], F32, name="sq%d" % s)
+            nc.scalar.activation(
+                out=sq[j, h, s][:, 256 * half : 256 * (half + 1)].rearrange("p (t q) -> p t q", t=2),
+                in_=zb[j, h, s][:].rearrange("p (q t) -> p t q", t=4)[:, 2 * half : 2 * half + 2, :],
+                func=ACT.Square,
+            )
+
+        def square(j, h, s):
+            t = work.tile([P, 512], F32, name="sq%d" % s)
+            sq[j, h, s] = t
+            if j == PAIRS - 1:
+                nc.scalar.activation(
+                    out=t[:].rearrange("p (t q) -> p t q", t=4),
+                    in_=zb[j, h, s][:].rearrange("p (q t) -> p t q", t=4),
+                    func=ACT.Square,
+                )
+                return
+            nc.scalar.activation(
+                out=t[:].rearrange("p (u q e) -> p u q e", u=2, e=2),
+                in_=zb[j, h, s][:].rearrange("p (q u e) -> p u q e", u=2, e=2),
+                func=ACT.Square,
+            )
+
+        def add(j, h, u0=0, u1=2):
+            if u0 == 0:
+                pw[j, h] = work.tile([P, 512], F32, name="pw")
+            c = slice(256 * u0, 256 * u1)
+            nc.vector.tensor_tensor(out=pw[j, h][:, c], in0=sq[j, h, 0][:, c], in1=sq[j, h, 1][:, c], op=ALU.add)
+
+        def gain(j, h, u0=0, u1=2):
+            if u0 == 0:
+                e[j, h] = work.tile([P, 512], BF16, name="e%d" % h)
+            b = j // 2
+            nc.vector.tensor_tensor(
+                out=e[j, h][:, 256 * u0 : 256 * u1],
+                in0=pw[j, h][:, 256 * u0 : 256 * u1],
+                in1=vb[:, 512 * b + 256 * u0 : 512 * b + 256 * u1],
+                op=ALU.mult,
+            )
+
+        acc = {}
+
+        def t_acc(j, h, t0, t1):
+            if t0 == 0:
+                acc[j, h] = bank("xt%d" % h)
+            for t in range(t0, t1):
+                c = slice(P * t, P * (t + 1))
+                for s in range(2):
+                    nc.tensor.matmul(
+                        acc[j, h][:, c], lhsT=sq[j, h, s][:, c], rhs=ident[:], start=(s == 0), stop=(s == 1), is_transpose=True
+                    )
+
+        def gain_acc(j, h):
+            if j not in eg:
+                eg[j] = work.tile([P, 1024], BF16, name="eg", align_bytes=64)
+            nc.vector.tensor_tensor(
+                out=eg[j][:, 512 * h : 512 * (h + 1)].rearrange("p (r t) -> p r t", t=4),
+                in0=acc[j, h][:].rearrange("p (t r) -> p r t", t=4),
+                in1=vcol[:].unsqueeze(1).to_broadcast([P, P, 4]),
+                op=ALU.mult,
+            )
+
+        def v_mm(i):
+            t = psum.tile([P, 1024], BF16, name=o_name())
+            vbank[i] = t
+            for k in range(2):
+                c = (2 * i + k) * A
+                nc.tensor.matmul(t[:, A * k : A * (k + 1)], lhsT=ones[:], rhs=vrow[:, c : c + A], start=True, stop=True)
+
+        def copy_v(i, eng):
+            dst = vb[:, 1024 * i : 1024 * (i + 1)].rearrange("p (b u q e) -> p b u q e", b=2, u=2, e=2)
+            src = vbank[i][:].rearrange("p (b q u e) -> p b u q e", b=2, u=2, e=2)
+            for k in range(2):
+                if eng is nc.scalar:
+                    nc.scalar.copy(out=dst[:, k], in_=src[:, k])
+                else:
+                    nc.vector.tensor_copy(out=dst[:, k], in_=src[:, k])
+
+        def t_e(j, h, u0=0, u1=2):
+            if j not in et:
+                et[j] = bank("et")
+            words = e[j, h][:].bitcast(F32)
+            for u in range(u0, u1):
+                c = (2 * h + u) * P
+                nc.tensor.transpose(et[j][:, c : c + P], words[:, P * u : P * (u + 1)], ident[:])
+
+        def copy_e(j, eng):
+            eg[j] = work.tile([P, 1024], BF16, name="eg", align_bytes=64)
+            dst = eg[j][:].bitcast(F32).rearrange("p (h r u) -> p h r u", h=2, u=2)
+            src = et[j][:].rearrange("p (h u r) -> p h r u", h=2, u=2)
+            if eng is nc.scalar:
+                nc.scalar.copy(out=dst, in_=src)
+            else:
+                nc.vector.tensor_copy(out=dst, in_=src)
+
+        def q_e(j, h0, h1):
+            if j not in ec:
+                ec[j] = work.tile([P, 256], U32, name="ec", align_bytes=64)
+                es[j] = work.tile([P, 256], U8, name="es", align_bytes=64)
+            nc.vector.quantize_mx(
+                out=ec[j][:, 128 * h0 : 128 * h1].bitcast(FP8X4),
+                scales=es[j][:, 128 * h0 : 128 * h1],
+                in_=eg[j][:, 512 * h0 : 512 * h1],
+            )
+
+        def m2(j, h):
+            b = j // 2
+            t = o_bank()
+            ob[j, h] = t
+            nc.tensor.matmul_mx(
+                out=t[:],
+                lhsT=ec[j][:, P * h : P * (h + 1)].bitcast(FP8X4),
+                lhsT_scale=es[j][:, P * h : P * (h + 1)],
+                rhs=sw[:, b, :].bitcast(FP4X4),
+                rhs_scale=splane[:, N * b : N * (b + 1)],
+                start=True,
+                stop=True,
+            )
+
+        def m2_part(j, h, n):
+            b = j // 2
+            t = z_bank()
+            ob[j, h, n] = t
+            nc.tensor.matmul_mx(
+                out=t[:, 0:256],
+                lhsT=ec[j][:, P * h : P * (h + 1)].bitcast(FP8X4),
+                lhsT_scale=es[j][:, P * h : P * (h + 1)],
+                rhs=sw[:, b, 512 * n : 512 * (n + 1)].bitcast(FP4X4),
+                rhs_scale=splane[:, N * b + 256 * n : N * b + 256 * (n + 1)],
+                start=True,
+                stop=True,
+            )
+
+        def copy_o_part(j, h, n, eng):
+            c = slice(256 * n, 256 * (n + 1))
+            if j not in osb:
+                osb[j] = work.tile([P, 2, N], F32, name="osb")
+            if eng is nc.scalar:
+                nc.scalar.copy(out=osb[j][:, h, c], in_=ob[j, h, n][:, 0:256])
+            else:
+                nc.vector.tensor_copy(out=osb[j][:, h, c], in_=ob[j, h, n][:, 0:256])
+            r0 = (j % 2) * 256 + 128 * h
+            nc.sync.dma_start(out=out[j // 2, r0 : r0 + 128, c], in_=osb[j][:, h, c])
+
+        def copy_o(j, h, eng):
+            if j not in osb:
+                osb[j] = work.tile([P, 2, N], F32, name="osb")
+            if eng is nc.scalar:
+                nc.scalar.copy(out=osb[j][:, h, :], in_=ob[j, h][:])
+            else:
+                nc.vector.tensor_copy(out=osb[j][:, h, :], in_=ob[j, h][:])
+            stored[j] = stored.get(j, 0) + 1
+            if j == PAIRS - 1:
+                store(j, h, h + 1)
+            elif stored[j] == 2:
+                store(j, 0, 2)
+
+        stored = {}
+
+        def store(j, h0, h1):
+            r0 = (j % 2) * 256
+            nc.sync.dma_start(
+                out=out[j // 2, r0 + 128 * h0 : r0 + 128 * h1, :].rearrange("(h p) n -> p h n", p=P),
+                in_=osb[j][:, h0:h1, :],
+            )
+
+        t_x(0, 0)
+        t_x(0, 1)
+        copy_x(0, 0, nc.vector)
+        v_mm(1)
+        t_x(1, 1)
+        v_mm(0)
+        copy_x(0, 1, nc.vector)
+        q_x(0, 0, 1)
+        copy_v(0, nc.scalar)
+        t_x(1, 0)
+        m1(0, 0, 0)
+        copy_v(1, nc.scalar)
+        copy_x(1, 1, nc.vector)
+        square(0, 0, 0)
+        q_x(0, 1, 2)
+        m1(0, 1, 0)
+        m1(0, 1, 1)
+        square(0, 1, 0)
+        m1(0, 0, 1)
+        square(0, 1, 1)
+        copy_x(1, 0, nc.vector)
+        q_x(1, 0, 2)
+        square(0, 0, 1)
+        t_x(2, 0)
+        add(0, 0)
+        t_x(2, 1)
+        copy_x(2, 0, nc.scalar)
+        add(0, 1)
+        gain(0, 0)
+        m1(1, 0, 1)
+        copy_x(2, 1, nc.vector)
+        m1(1, 0, 0)
+        gain(0, 1)
+        square(1, 0, 1)
+        square(1, 0, 0)
+        m1(1, 1, 0)
+        square(1, 1, 0)
+        q_x(2, 0, 2)
+        m1(1, 1, 1)
+        t_x(3, 0)
+        square(1, 1, 1)
+        add(1, 0)
+        t_x(3, 1)
+        copy_x(3, 0, nc.scalar)
+        t_e(0, 0)
+        t_e(0, 1)
+        add(1, 1)
+        gain(1, 0)
+        m1(2, 0, 1)
+        copy_x(3, 1, nc.scalar)
+        copy_e(0, nc.vector)
+        m1(2, 0, 0)
+        gain(1, 1)
+        square(2, 0, 1)
+        square(2, 0, 0)
+        m1(2, 1, 0)
+        square(2, 1, 0)
+        q_x(3, 0, 2)
+        m1(2, 1, 1)
+        t_x(4, 0)
+        q_e(0, 0, 2)
+        square(2, 1, 1)
+        add(2, 0)
+        t_x(4, 1)
+        copy_x(4, 0, nc.scalar)
+        t_e(1, 0)
+        t_e(1, 1)
+        add(2, 1)
+        gain(2, 0)
+        m1(3, 0, 1)
+        m2(0, 1)
+        copy_x(4, 1, nc.scalar)
+        copy_e(1, nc.scalar)
+        m1(3, 0, 0)
+        gain(2, 1)
+        square(3, 0, 1)
+        m2(0, 0)
+        square(3, 0, 0)
+        m1(3, 1, 0)
+        square(3, 1, 0)
+        q_x(4, 0, 2)
+        m1(3, 1, 1)
+        copy_o(0, 0, nc.scalar)
+        t_x(5, 0)
+        q_e(1, 0, 2)
+        square(3, 1, 1)
+        add(3, 0)
+        copy_o(0, 1, nc.vector)
+        t_x(5, 1)
+        copy_x(5, 0, nc.vector)
+        t_e(2, 0)
+        t_e(2, 1)
+        add(3, 1)
+        gain(3, 0)
+        m1(4, 0, 1)
+        m2(1, 1)
+        copy_x(5, 1, nc.scalar)
+        copy_e(2, nc.scalar)
+        m1(4, 0, 0)
+        gain(3, 1)
+        square(4, 0, 1)
+        m2(1, 0)
+        square(4, 0, 0)
+        m1(4, 1, 0)
+        square(4, 1, 0)
+        q_x(5, 0, 2)
+        m1(4, 1, 1)
+        copy_o(1, 0, nc.vector)
+        t_x(6, 0)
+        q_e(2, 0, 2)
+        square(4, 1, 1)
+        add(4, 0)
+        copy_o(1, 1, nc.scalar)
+        t_x(6, 1)
+        copy_x(6, 0, nc.scalar)
+        t_e(3, 0)
+        t_e(3, 1)
+        add(4, 1)
+        gain(4, 0)
+        m1(5, 0, 1)
+        m2(2, 1)
+        copy_x(6, 1, nc.vector)
+        copy_e(3, nc.scalar)
+        m1(5, 0, 0)
+        gain(4, 1)
+        square(5, 0, 1)
+        m2(2, 0)
+        square(5, 0, 0)
+        m1(5, 1, 0)
+        square(5, 1, 0)
+        q_x(6, 0, 2)
+        m1(5, 1, 1)
+        copy_o(2, 0, nc.vector)
+        q_e(3, 0, 2)
+        square(5, 1, 1)
+        add(5, 0)
+        copy_o(2, 1, nc.scalar)
+        t_e(4, 0)
+        t_x(7, 0)
+        t_x(7, 1)
+        t_e(4, 1)
+        add(5, 1)
+        gain(5, 0)
+        copy_x(7, 0, nc.vector)
+        copy_x(7, 1, nc.scalar)
+        m1(6, 0, 1)
+        m2(3, 1)
+        copy_e(4, nc.scalar)
+        m1(6, 0, 0)
+        gain(5, 1)
+        square(6, 0, 1)
+        m2(3, 0)
+        square(6, 0, 0)
+        m1(6, 1, 0)
+        q_x(7, 0, 2)
+        square(6, 1, 0)
+        m1(6, 1, 1)
+        m1(7, 1, 0)
+        copy_o(3, 0, nc.vector)
+        q_e(4, 0, 2)
+        square(6, 1, 1)
+        add(6, 0)
+        copy_o(3, 1, nc.scalar)
+        t_e(5, 0)
+        t_e(5, 1)
+        add(6, 1)
+        m1(7, 1, 1)
+        gain(6, 0)
+        m2(4, 1)
+        copy_e(5, nc.scalar)
+        gain(6, 1)
+        m2(4, 0)
+        square(7, 1, 0)
+        m1(7, 0, 1)
+        copy_o(4, 0, nc.vector)
+        q_e(5, 0, 2)
+        copy_o(4, 1, nc.scalar)
+        m1(7, 0, 0)
+        t_e(6, 0)
+        t_e(6, 1)
+        copy_e(6, nc.vector)
+        square_part(7, 1, 1, 0)
+        square_part(7, 1, 1, 1)
+        t_acc(7, 1, 0, 2)
+        square(7, 0, 1)
+        t_acc(7, 1, 2, 4)
+        m2(5, 1)
+        square(7, 0, 0)
+        m2(5, 0)
+        gain_acc(7, 1)
+        t_acc(7, 0, 0, 4)
+        copy_o(5, 1, nc.scalar)
+        q_e(6, 0, 2)
+        q_e(7, 1, 2)
+        copy_o(5, 0, nc.scalar)
+        m2(6, 0)
+        copy_o(6, 0, nc.scalar)
+        m2_part(7, 1, 1)
+        copy_o_part(7, 1, 1, nc.scalar)
+        gain_acc(7, 0)
+        m2(6, 1)
+        q_e(7, 0, 1)
+        m2_part(7, 1, 0)
+        m2(7, 0)
+        copy_o(6, 1, nc.vector)
+        copy_o(7, 0, nc.scalar)
+        copy_o_part(7, 1, 0, nc.vector)

@@ -26,7 +26,7 @@ def tile_cyclostationary_band_detector_s14_kernel(tc, x, basis_words, basis_scal
     nc = tc.nc
     with ExitStack() as ctx:
         keep = ctx.enter_context(tc.tile_pool(name="keep", bufs=1))
-        work = ctx.enter_context(tc.tile_pool(name="work", bufs=6))
+        work = ctx.enter_context(tc.tile_pool(name="work", bufs=5))
         psum = ctx.enter_context(tc.psum_pool(name="psum", bufs=1))
         ctx.enter_context(tc.manual_schedule())
 
@@ -66,19 +66,19 @@ def tile_cyclostationary_band_detector_s14_kernel(tc, x, basis_words, basis_scal
                 in_=src[:, r:16:4, :].bitcast(I32).rearrange("g q n -> q g n"),
             )
 
-        nc.scalar.dma_start(out=vrow[0:1, :], in_=v.rearrange("(o b) a -> o (b a)", o=1))
+        nc.gpsimd.dma_start(out=vrow[0:1, :], in_=v.rearrange("(o b) a -> o (b a)", o=1))
+        nc.gpsimd.dma_start(out=vcol[:], in_=v[G - 1].rearrange("(p t) -> p t", t=4))
         load_x(0, 0)
         load_x(0, 1)
         for r in range(4):
-            load_scales(plane0, basis_scales[0:2], r, nc.scalar if r < 2 else nc.gpsimd)
+            load_scales(plane0, basis_scales[0:2], r, nc.scalar)
         load_x_pair(1)
-        for g in range(2):
-            nc.sync.dma_start(out=bw[0][:, g, :], in_=basis_words[g])
+        nc.sync.dma_start(out=bw[0][:], in_=basis_words[0:2].rearrange("g p n -> p g n"))
         load_x_pair(2)
         for r in range(4):
-            load_scales(plane1, basis_scales[2:8], r, nc.gpsimd)
+            load_scales(plane1, basis_scales[2:8], r, nc.sync)
         for r in range(4):
-            load_scales(splane, sig_scales, r, nc.gpsimd)
+            load_scales(splane, sig_scales, r, nc.sync)
         for b in range(1, G):
             nc.sync.dma_start(out=bw[b][:], in_=basis_words[2 * b : 2 * b + 2].rearrange("g p n -> p g n"))
             load_x_pair(2 * b + 1)
@@ -86,7 +86,6 @@ def tile_cyclostationary_band_detector_s14_kernel(tc, x, basis_words, basis_scal
                 nc.sync.dma_start(out=sw[:], in_=sig_words.rearrange("b p n -> p b n"))
             if b + 1 < G:
                 load_x_pair(2 * b + 2)
-        nc.sync.dma_start(out=vcol[:], in_=v[G - 1].rearrange("(p t) -> p t", t=4))
 
         def basis_plane(b):
             return plane0[:] if b == 0 else plane1[:, 2048 * (b - 1) : 2048 * b]
@@ -122,7 +121,19 @@ def tile_cyclostationary_band_detector_s14_kernel(tc, x, basis_words, basis_scal
             for g in range(2):
                 for u in range(2):
                     c = (2 * g + u) * P
+                    if j in xu:
+                        nc.tensor.transpose(t[:, c : c + P], xu[j][:, h, c : c + P], ident[:])
+                        continue
                     nc.tensor.transpose(t[:, c : c + P], words[:, 256 * g + u : 256 * (g + 1) : 2], ident[:])
+
+        xu = {}
+
+        def u_x(j):
+            xu[j] = work.tile([P, 2, 512], F32, name="xu")
+            nc.vector.tensor_copy(
+                out=xu[j][:].rearrange("p h (g u q) -> p (h g) u q", g=2, u=2),
+                in_=x_sb[j][:].rearrange("p h k -> p (h k)").bitcast(F32).rearrange("p (m q u) -> p m u q", m=4, u=2),
+            )
 
         def copy_x(j, h, eng):
             if j not in xg:
@@ -160,45 +171,43 @@ def tile_cyclostationary_band_detector_s14_kernel(tc, x, basis_words, basis_scal
                     stop=(g == 1),
                 )
 
+        def sq_tile(j, h, s):
+            if (j, s) not in sq:
+                sq[j, s] = work.tile([P, 2, 512], F32, name="sq%d" % s)
+            return sq[j, s][:, h, :]
+
         def square_part(j, h, s, half):
-            if half == 0:
-                sq[j, h, s] = work.tile([P, 512], F32, name="sq%d" % s)
             nc.scalar.activation(
-                out=sq[j, h, s][:, 256 * half : 256 * (half + 1)].rearrange("p (t q) -> p t q", t=2),
+                out=sq_tile(j, h, s)[:, 256 * half : 256 * (half + 1)].rearrange("p (t q) -> p t q", t=2),
                 in_=zb[j, h, s][:].rearrange("p (q t) -> p t q", t=4)[:, 2 * half : 2 * half + 2, :],
                 func=ACT.Square,
             )
 
         def square(j, h, s):
-            t = work.tile([P, 512], F32, name="sq%d" % s)
-            sq[j, h, s] = t
             if j == PAIRS - 1:
                 nc.scalar.activation(
-                    out=t[:].rearrange("p (t q) -> p t q", t=4),
+                    out=sq_tile(j, h, s).rearrange("p (t q) -> p t q", t=4),
                     in_=zb[j, h, s][:].rearrange("p (q t) -> p t q", t=4),
                     func=ACT.Square,
                 )
                 return
             nc.scalar.activation(
-                out=t[:].rearrange("p (u q e) -> p u q e", u=2, e=2),
+                out=sq_tile(j, h, s).rearrange("p (u q e) -> p u q e", u=2, e=2),
                 in_=zb[j, h, s][:].rearrange("p (q u e) -> p u q e", u=2, e=2),
                 func=ACT.Square,
             )
 
-        def add(j, h, u0=0, u1=2):
-            if u0 == 0:
-                pw[j, h] = work.tile([P, 512], F32, name="pw")
-            c = slice(256 * u0, 256 * u1)
-            nc.vector.tensor_tensor(out=pw[j, h][:, c], in0=sq[j, h, 0][:, c], in1=sq[j, h, 1][:, c], op=ALU.add)
+        def add(j):
+            pw[j] = work.tile([P, 2, 512], F32, name="pw")
+            nc.vector.tensor_tensor(out=pw[j][:], in0=sq[j, 0][:], in1=sq[j, 1][:], op=ALU.add)
 
-        def gain(j, h, u0=0, u1=2):
-            if u0 == 0:
-                e[j, h] = work.tile([P, 512], BF16, name="e%d" % h)
+        def gain(j):
+            e[j] = work.tile([P, 2, 512], BF16, name="e")
             b = j // 2
             nc.vector.tensor_tensor(
-                out=e[j, h][:, 256 * u0 : 256 * u1],
-                in0=pw[j, h][:, 256 * u0 : 256 * u1],
-                in1=vb[:, 512 * b + 256 * u0 : 512 * b + 256 * u1],
+                out=e[j][:],
+                in0=pw[j][:],
+                in1=vb[:, 512 * b : 512 * (b + 1)].unsqueeze(1).to_broadcast([P, 2, 512]),
                 op=ALU.mult,
             )
 
@@ -211,7 +220,7 @@ def tile_cyclostationary_band_detector_s14_kernel(tc, x, basis_words, basis_scal
                 c = slice(P * t, P * (t + 1))
                 for s in range(2):
                     nc.tensor.matmul(
-                        acc[j, h][:, c], lhsT=sq[j, h, s][:, c], rhs=ident[:], start=(s == 0), stop=(s == 1), is_transpose=True
+                        acc[j, h][:, c], lhsT=sq[j, s][:, h, c], rhs=ident[:], start=(s == 0), stop=(s == 1), is_transpose=True
                     )
 
         def gain_acc(j, h):
@@ -243,7 +252,7 @@ def tile_cyclostationary_band_detector_s14_kernel(tc, x, basis_words, basis_scal
         def t_e(j, h, u0=0, u1=2):
             if j not in et:
                 et[j] = bank("et")
-            words = e[j, h][:].bitcast(F32)
+            words = e[j][:, h, :].bitcast(F32)
             for u in range(u0, u1):
                 c = (2 * h + u) * P
                 nc.tensor.transpose(et[j][:, c : c + P], words[:, P * u : P * (u + 1)], ident[:])
@@ -313,13 +322,7 @@ def tile_cyclostationary_band_detector_s14_kernel(tc, x, basis_words, basis_scal
                 nc.scalar.copy(out=osb[j][:, h, :], in_=ob[j, h][:])
             else:
                 nc.vector.tensor_copy(out=osb[j][:, h, :], in_=ob[j, h][:])
-            stored[j] = stored.get(j, 0) + 1
-            if j == PAIRS - 1:
-                store(j, h, h + 1)
-            elif stored[j] == 2:
-                store(j, 0, 2)
-
-        stored = {}
+            store(j, h, h + 1)
 
         def store(j, h0, h1):
             r0 = (j % 2) * 256
@@ -330,208 +333,194 @@ def tile_cyclostationary_band_detector_s14_kernel(tc, x, basis_words, basis_scal
 
         t_x(0, 0)
         t_x(0, 1)
-        copy_x(0, 0, nc.vector)
+        copy_x(0, 0, nc.scalar)
+        copy_x(0, 1, nc.scalar)
         v_mm(1)
-        t_x(1, 1)
         v_mm(0)
-        copy_x(0, 1, nc.vector)
+        t_x(1, 1)
         q_x(0, 0, 1)
-        copy_v(0, nc.scalar)
+        copy_x(1, 1, nc.scalar)
         t_x(1, 0)
-        m1(0, 0, 0)
         copy_v(1, nc.scalar)
-        copy_x(1, 1, nc.vector)
-        square(0, 0, 0)
         q_x(0, 1, 2)
-        m1(0, 1, 0)
+        m1(0, 0, 0)
         m1(0, 1, 1)
-        square(0, 1, 0)
-        m1(0, 0, 1)
+        copy_v(0, nc.vector)
+        square(0, 0, 0)
+        m1(0, 1, 0)
         square(0, 1, 1)
         copy_x(1, 0, nc.vector)
-        q_x(1, 0, 2)
+        square(0, 1, 0)
+        m1(0, 0, 1)
         square(0, 0, 1)
-        t_x(2, 0)
-        add(0, 0)
+        q_x(1, 0, 2)
         t_x(2, 1)
-        copy_x(2, 0, nc.scalar)
-        add(0, 1)
-        gain(0, 0)
+        t_x(2, 0)
         m1(1, 0, 1)
-        copy_x(2, 1, nc.vector)
         m1(1, 0, 0)
-        gain(0, 1)
-        square(1, 0, 1)
-        square(1, 0, 0)
-        m1(1, 1, 0)
-        square(1, 1, 0)
-        q_x(2, 0, 2)
         m1(1, 1, 1)
-        t_x(3, 0)
+        copy_x(2, 1, nc.scalar)
+        add(0)
+        square(1, 0, 1)
+        m1(1, 1, 0)
+        copy_x(2, 0, nc.vector)
+        square(1, 0, 0)
         square(1, 1, 1)
-        add(1, 0)
         t_x(3, 1)
-        copy_x(3, 0, nc.scalar)
-        t_e(0, 0)
+        gain(0)
+        t_x(3, 0)
+        square(1, 1, 0)
         t_e(0, 1)
-        add(1, 1)
-        gain(1, 0)
+        t_e(0, 0)
+        q_x(2, 0, 2)
         m1(2, 0, 1)
-        copy_x(3, 1, nc.scalar)
-        copy_e(0, nc.vector)
         m1(2, 0, 0)
-        gain(1, 1)
-        square(2, 0, 1)
-        square(2, 0, 0)
-        m1(2, 1, 0)
-        square(2, 1, 0)
-        q_x(3, 0, 2)
         m1(2, 1, 1)
-        t_x(4, 0)
-        q_e(0, 0, 2)
+        copy_x(3, 1, nc.scalar)
+        copy_e(0, nc.scalar)
+        add(1)
+        square(2, 0, 1)
+        m1(2, 1, 0)
+        copy_x(3, 0, nc.vector)
+        square(2, 0, 0)
         square(2, 1, 1)
-        add(2, 0)
         t_x(4, 1)
-        copy_x(4, 0, nc.scalar)
-        t_e(1, 0)
+        gain(1)
+        t_x(4, 0)
+        square(2, 1, 0)
         t_e(1, 1)
-        add(2, 1)
-        gain(2, 0)
+        t_e(1, 0)
+        q_e(0, 0, 2)
+        q_x(3, 0, 2)
         m1(3, 0, 1)
+        m1(3, 0, 0)
+        m1(3, 1, 1)
         m2(0, 1)
         copy_x(4, 1, nc.scalar)
-        copy_e(1, nc.scalar)
-        m1(3, 0, 0)
-        gain(2, 1)
-        square(3, 0, 1)
         m2(0, 0)
-        square(3, 0, 0)
+        copy_e(1, nc.scalar)
+        add(2)
+        square(3, 0, 1)
         m1(3, 1, 0)
-        square(3, 1, 0)
-        q_x(4, 0, 2)
-        m1(3, 1, 1)
-        copy_o(0, 0, nc.scalar)
-        t_x(5, 0)
-        q_e(1, 0, 2)
+        copy_x(4, 0, nc.vector)
+        square(3, 0, 0)
         square(3, 1, 1)
-        add(3, 0)
-        copy_o(0, 1, nc.vector)
         t_x(5, 1)
-        copy_x(5, 0, nc.vector)
-        t_e(2, 0)
+        copy_o(0, 1, nc.scalar)
+        gain(2)
+        t_x(5, 0)
+        square(3, 1, 0)
         t_e(2, 1)
-        add(3, 1)
-        gain(3, 0)
+        t_e(2, 0)
+        q_e(1, 0, 2)
+        q_x(4, 0, 2)
+        copy_o(0, 0, nc.vector)
         m1(4, 0, 1)
+        m1(4, 0, 0)
+        m1(4, 1, 1)
         m2(1, 1)
         copy_x(5, 1, nc.scalar)
-        copy_e(2, nc.scalar)
-        m1(4, 0, 0)
-        gain(3, 1)
-        square(4, 0, 1)
         m2(1, 0)
-        square(4, 0, 0)
+        copy_e(2, nc.scalar)
+        add(3)
+        square(4, 0, 1)
         m1(4, 1, 0)
-        square(4, 1, 0)
-        q_x(5, 0, 2)
-        m1(4, 1, 1)
-        copy_o(1, 0, nc.vector)
-        t_x(6, 0)
-        q_e(2, 0, 2)
+        copy_x(5, 0, nc.vector)
+        square(4, 0, 0)
         square(4, 1, 1)
-        add(4, 0)
-        copy_o(1, 1, nc.scalar)
         t_x(6, 1)
-        copy_x(6, 0, nc.scalar)
-        t_e(3, 0)
+        copy_o(1, 1, nc.scalar)
+        gain(3)
+        t_x(6, 0)
+        square(4, 1, 0)
         t_e(3, 1)
-        add(4, 1)
-        gain(4, 0)
+        t_e(3, 0)
+        q_e(2, 0, 2)
+        q_x(5, 0, 2)
+        copy_o(1, 0, nc.vector)
         m1(5, 0, 1)
-        m2(2, 1)
-        copy_x(6, 1, nc.vector)
-        copy_e(3, nc.scalar)
         m1(5, 0, 0)
-        gain(4, 1)
-        square(5, 0, 1)
-        m2(2, 0)
-        square(5, 0, 0)
-        m1(5, 1, 0)
-        square(5, 1, 0)
-        q_x(6, 0, 2)
         m1(5, 1, 1)
-        copy_o(2, 0, nc.vector)
-        q_e(3, 0, 2)
-        square(5, 1, 1)
-        add(5, 0)
-        copy_o(2, 1, nc.scalar)
-        t_e(4, 0)
-        t_x(7, 0)
+        m2(2, 1)
+        copy_x(6, 1, nc.scalar)
+        m2(2, 0)
+        copy_e(3, nc.scalar)
+        add(4)
+        square(5, 0, 1)
+        m1(5, 1, 0)
+        copy_x(6, 0, nc.vector)
         t_x(7, 1)
+        t_x(7, 0)
+        square(5, 0, 0)
+        square(5, 1, 1)
+        copy_o(2, 1, nc.scalar)
+        gain(4)
+        square(5, 1, 0)
         t_e(4, 1)
-        add(5, 1)
-        gain(5, 0)
-        copy_x(7, 0, nc.vector)
-        copy_x(7, 1, nc.scalar)
+        t_e(4, 0)
+        q_e(3, 0, 2)
+        q_x(6, 0, 2)
+        copy_o(2, 0, nc.vector)
         m1(6, 0, 1)
-        m2(3, 1)
-        copy_e(4, nc.scalar)
         m1(6, 0, 0)
-        gain(5, 1)
-        square(6, 0, 1)
+        copy_x(7, 1, nc.scalar)
+        m1(6, 1, 1)
+        m2(3, 1)
         m2(3, 0)
-        square(6, 0, 0)
+        copy_e(4, nc.scalar)
+        add(5)
+        square(6, 0, 1)
+        copy_x(7, 0, nc.vector)
         m1(6, 1, 0)
+        square(6, 0, 0)
+        square(6, 1, 1)
+        copy_o(3, 1, nc.scalar)
+        gain(5)
         q_x(7, 0, 2)
         square(6, 1, 0)
-        m1(6, 1, 1)
-        m1(7, 1, 0)
-        copy_o(3, 0, nc.vector)
-        q_e(4, 0, 2)
-        square(6, 1, 1)
-        add(6, 0)
-        copy_o(3, 1, nc.scalar)
-        t_e(5, 0)
         t_e(5, 1)
-        add(6, 1)
-        m1(7, 1, 1)
-        gain(6, 0)
+        t_e(5, 0)
+        q_e(4, 0, 2)
+        copy_o(3, 0, nc.vector)
+        m1(7, 1, 0)
         m2(4, 1)
-        copy_e(5, nc.scalar)
-        gain(6, 1)
         m2(4, 0)
+        copy_e(5, nc.scalar)
+        m1(7, 1, 1)
+        add(6)
         square(7, 1, 0)
-        m1(7, 0, 1)
-        copy_o(4, 0, nc.vector)
-        q_e(5, 0, 2)
         copy_o(4, 1, nc.scalar)
-        m1(7, 0, 0)
-        t_e(6, 0)
-        t_e(6, 1)
-        copy_e(6, nc.vector)
+        gain(6)
+        q_e(5, 0, 2)
+        copy_o(4, 0, nc.vector)
         square_part(7, 1, 1, 0)
+        m1(7, 0, 1)
         square_part(7, 1, 1, 1)
-        t_acc(7, 1, 0, 2)
+        m1(7, 0, 0)
         square(7, 0, 1)
+        t_acc(7, 1, 0, 2)
+        t_e(6, 1)
         t_acc(7, 1, 2, 4)
-        m2(5, 1)
         square(7, 0, 0)
-        m2(5, 0)
+        t_e(6, 0)
+        copy_e(6, nc.scalar)
         gain_acc(7, 1)
-        t_acc(7, 0, 0, 4)
-        copy_o(5, 1, nc.scalar)
-        q_e(6, 0, 2)
         q_e(7, 1, 2)
-        copy_o(5, 0, nc.scalar)
-        m2(6, 0)
-        copy_o(6, 0, nc.scalar)
-        m2_part(7, 1, 1)
-        copy_o_part(7, 1, 1, nc.scalar)
+        q_e(6, 0, 2)
+        m2(5, 1)
+        t_acc(7, 0, 0, 4)
         gain_acc(7, 0)
-        m2(6, 1)
         q_e(7, 0, 1)
-        m2_part(7, 1, 0)
+        m2(5, 0)
+        copy_o(5, 1, nc.scalar)
+        m2(6, 0)
+        copy_o(5, 0, nc.scalar)
+        m2_part(7, 1, 1)
+        copy_o(6, 0, nc.vector)
         m2(7, 0)
+        m2_part(7, 1, 0)
+        copy_o_part(7, 1, 1, nc.scalar)
+        copy_o_part(7, 1, 0, nc.scalar)
+        m2(6, 1)
+        copy_o(7, 0, nc.vector)
         copy_o(6, 1, nc.vector)
-        copy_o(7, 0, nc.scalar)
-        copy_o_part(7, 1, 0, nc.vector)

@@ -18,8 +18,8 @@ ALU = mybir.AluOpType
 
 P = 128
 PAIRS = G * M // 256
-Z_BANKS = 3
-O_BANKS = 2
+WARM = 5
+RING = {"x": 2, "z": 3, "o": 2, "e": 1}
 
 
 def tile_cyclostationary_band_detector_s14_kernel(tc, x, basis_words, basis_scales, v, sig_words, sig_scales, out):
@@ -38,6 +38,8 @@ def tile_cyclostationary_band_detector_s14_kernel(tc, x, basis_words, basis_scal
         vrow = keep.tile([P, G * A], BF16, name="vrow")
         ones = keep.tile([P, P], BF16, name="ones")
         ident = keep.tile([P, P], F32, name="ident")
+        warm = keep.tile([P, 512], BF16, name="warm")
+        nc.vector.memset(warm[:].bitcast(I32), 0)
         vb = keep.tile([P, G * A], BF16, name="vb")
         vcol = keep.tile([P, 4], BF16, name="vcol")
         nc.vector.memset(vrow[:].bitcast(I32), 0)
@@ -49,7 +51,7 @@ def tile_cyclostationary_band_detector_s14_kernel(tc, x, basis_words, basis_scal
         nc.scalar.activation(out=dummy[:], in_=dummy[:], func=ACT.Square)
 
         x_sb = [keep.tile([P, 2, T], BF16, name="x%d" % j) for j in range(PAIRS)]
-        bw = [keep.tile([P, 2, 4 * A], U8, name="bw%d" % b, align_bytes=64) for b in range(G)]
+        bw = [[keep.tile([P, 2, 2 * A], U8, name="bw%d%d" % (b, s), align_bytes=64) for s in range(2)] for b in range(G)]
         sw = keep.tile([P, G, 2 * N], U8, name="sw", align_bytes=64)
 
         def load_x(j, h):
@@ -66,46 +68,44 @@ def tile_cyclostationary_band_detector_s14_kernel(tc, x, basis_words, basis_scal
                 in_=src[:, r:16:4, :].bitcast(I32).rearrange("g q n -> q g n"),
             )
 
+        def load_bw(b, s):
+            c = slice(2 * A * s, 2 * A * (s + 1))
+            nc.sync.dma_start(out=bw[b][s][:], in_=basis_words[2 * b : 2 * b + 2, :, c].rearrange("g p n -> p g n"))
+
         nc.gpsimd.dma_start(out=vrow[0:1, :], in_=v.rearrange("(o b) a -> o (b a)", o=1))
+        for r in range(4):
+            load_scales(plane1, basis_scales[2:8], r, nc.gpsimd)
+        for r in range(4):
+            load_scales(splane, sig_scales, r, nc.gpsimd)
         nc.gpsimd.dma_start(out=vcol[:], in_=v[G - 1].rearrange("(p t) -> p t", t=4))
         load_x(0, 0)
         load_x(0, 1)
         for r in range(4):
             load_scales(plane0, basis_scales[0:2], r, nc.scalar)
         load_x_pair(1)
-        nc.sync.dma_start(out=bw[0][:], in_=basis_words[0:2].rearrange("g p n -> p g n"))
+        load_bw(0, 0)
+        load_bw(0, 1)
         load_x_pair(2)
-        for r in range(4):
-            load_scales(plane1, basis_scales[2:8], r, nc.sync)
-        for r in range(4):
-            load_scales(splane, sig_scales, r, nc.sync)
+        load_x_pair(3)
         for b in range(1, G):
-            nc.sync.dma_start(out=bw[b][:], in_=basis_words[2 * b : 2 * b + 2].rearrange("g p n -> p g n"))
-            load_x_pair(2 * b + 1)
+            load_bw(b, 0)
+            load_bw(b, 1)
             if b == 1:
+                load_x_pair(4)
                 nc.sync.dma_start(out=sw[:], in_=sig_words.rearrange("b p n -> p b n"))
-            if b + 1 < G:
-                load_x_pair(2 * b + 2)
+                load_x_pair(5)
+            if b == 2:
+                load_x_pair(6)
+                load_x_pair(7)
 
         def basis_plane(b):
             return plane0[:] if b == 0 else plane1[:, 2048 * (b - 1) : 2048 * b]
 
-        z_count = [0]
-        o_count = [0]
+        turn = {"x": 0, "z": 0, "o": 0, "e": 0}
 
-        def bank(name):
-            return psum.tile([P, 512], F32, name=name)
-
-        def z_bank():
-            z_count[0] += 1
-            return bank("z%d" % (z_count[0] % Z_BANKS))
-
-        def o_name():
-            o_count[0] += 1
-            return "o%d" % (o_count[0] % O_BANKS)
-
-        def o_bank():
-            return bank(o_name())
+        def ring(kind, dtype=F32, width=512):
+            turn[kind] += 1
+            return psum.tile([P, width], dtype, name="%s%d" % (kind, turn[kind] % RING[kind]))
 
         vbank = {}
 
@@ -114,8 +114,12 @@ def tile_cyclostationary_band_detector_s14_kernel(tc, x, basis_words, basis_scal
         et, eg, ec, es = {}, {}, {}, {}
         ob, osb = {}, {}
 
+        for i in range(WARM):
+            wb = psum.tile([P, 512], F32, name="e0")
+            nc.tensor.matmul(wb[:], lhsT=warm[:, 0:P], rhs=warm[:], start=True, stop=True)
+
         def t_x(j, h):
-            t = bank("xt%d" % h)
+            t = ring("x")
             xt[j, h] = t
             words = x_sb[j][:, h, :].bitcast(F32)
             for g in range(2):
@@ -157,7 +161,7 @@ def tile_cyclostationary_band_detector_s14_kernel(tc, x, basis_words, basis_scal
 
         def m1(j, h, s):
             b = j // 2
-            t = z_bank()
+            t = ring("z")
             zb[j, h, s] = t
             for g in range(2):
                 c = (2 * h + g) * P
@@ -165,11 +169,40 @@ def tile_cyclostationary_band_detector_s14_kernel(tc, x, basis_words, basis_scal
                     out=t[:],
                     lhsT=xc[j][:, c : c + P].bitcast(FP8X4),
                     lhsT_scale=xs[j][:, c : c + P],
-                    rhs=bw[b][:, g, 1024 * s : 1024 * (s + 1)].bitcast(FP4X4),
+                    rhs=bw[b][s][:, g, :].bitcast(FP4X4),
                     rhs_scale=basis_plane(b)[:, 1024 * g + 512 * s : 1024 * g + 512 * (s + 1)],
                     start=(g == 0),
                     stop=(g == 1),
                 )
+
+        def t_x0(h, g):
+            t = ring("x")
+            xt[0, h, g] = t
+            words = x_sb[0][:, h, :].bitcast(F32)
+            for u in range(2):
+                nc.tensor.transpose(t[:, P * u : P * (u + 1)], words[:, 256 * g + u : 256 * (g + 1) : 2], ident[:])
+
+        def copy_x0(h, g, eng):
+            if 0 not in xg:
+                xg[0] = work.tile([P, 2048], BF16, name="xg", align_bytes=64)
+            c = 512 * (2 * h + g)
+            dst = xg[0][:, c : c + 512].bitcast(F32).rearrange("p (r u) -> p r u", u=2)
+            src = xt[0, h, g][:, 0:256].rearrange("p (u r) -> p r u", u=2)
+            if eng is nc.scalar:
+                nc.scalar.copy(out=dst, in_=src)
+            else:
+                nc.vector.tensor_copy(out=dst, in_=src)
+
+        def q_x0(h, g):
+            if 0 not in xc:
+                xc[0] = work.tile([P, 512], U32, name="xc", align_bytes=64)
+                xs[0] = work.tile([P, 512], U8, name="xs", align_bytes=64)
+            c = 2 * h + g
+            nc.vector.quantize_mx(
+                out=xc[0][:, 128 * c : 128 * (c + 1)].bitcast(FP8X4),
+                scales=xs[0][:, 128 * c : 128 * (c + 1)],
+                in_=xg[0][:, 512 * c : 512 * (c + 1)],
+            )
 
         def sq_tile(j, h, s):
             if (j, s) not in sq:
@@ -215,7 +248,7 @@ def tile_cyclostationary_band_detector_s14_kernel(tc, x, basis_words, basis_scal
 
         def t_acc(j, h, t0, t1):
             if t0 == 0:
-                acc[j, h] = bank("xt%d" % h)
+                acc[j, h] = ring("x")
             for t in range(t0, t1):
                 c = slice(P * t, P * (t + 1))
                 for s in range(2):
@@ -234,7 +267,7 @@ def tile_cyclostationary_band_detector_s14_kernel(tc, x, basis_words, basis_scal
             )
 
         def v_mm(i):
-            t = psum.tile([P, 1024], BF16, name=o_name())
+            t = ring("o", BF16, 1024)
             vbank[i] = t
             for k in range(2):
                 c = (2 * i + k) * A
@@ -251,7 +284,7 @@ def tile_cyclostationary_band_detector_s14_kernel(tc, x, basis_words, basis_scal
 
         def t_e(j, h, u0=0, u1=2):
             if j not in et:
-                et[j] = bank("et")
+                et[j] = ring("e")
             words = e[j][:, h, :].bitcast(F32)
             for u in range(u0, u1):
                 c = (2 * h + u) * P
@@ -278,7 +311,7 @@ def tile_cyclostationary_band_detector_s14_kernel(tc, x, basis_words, basis_scal
 
         def m2(j, h):
             b = j // 2
-            t = o_bank()
+            t = ring("o")
             ob[j, h] = t
             nc.tensor.matmul_mx(
                 out=t[:],
@@ -292,7 +325,7 @@ def tile_cyclostationary_band_detector_s14_kernel(tc, x, basis_words, basis_scal
 
         def m2_part(j, h, n):
             b = j // 2
-            t = z_bank()
+            t = ring("z")
             ob[j, h, n] = t
             nc.tensor.matmul_mx(
                 out=t[:, 0:256],
@@ -334,193 +367,197 @@ def tile_cyclostationary_band_detector_s14_kernel(tc, x, basis_words, basis_scal
         t_x(0, 0)
         t_x(0, 1)
         copy_x(0, 0, nc.scalar)
+        v_mm(0)
         copy_x(0, 1, nc.scalar)
         v_mm(1)
-        v_mm(0)
-        t_x(1, 1)
+        u_x(1)
+        copy_v(0, nc.scalar)
         q_x(0, 0, 1)
-        copy_x(1, 1, nc.scalar)
         t_x(1, 0)
-        copy_v(1, nc.scalar)
-        q_x(0, 1, 2)
+        copy_v(1, nc.vector)
+        t_x(1, 1)
         m1(0, 0, 0)
-        m1(0, 1, 1)
-        copy_v(0, nc.vector)
+        q_x(0, 1, 2)
+        copy_x(1, 0, nc.scalar)
+        copy_x(1, 1, nc.vector)
+        m1(0, 0, 1)
+        u_x(2)
         square(0, 0, 0)
         m1(0, 1, 0)
-        square(0, 1, 1)
-        copy_x(1, 0, nc.vector)
-        square(0, 1, 0)
-        m1(0, 0, 1)
-        square(0, 0, 1)
         q_x(1, 0, 2)
-        t_x(2, 1)
+        square(0, 0, 1)
+        m1(0, 1, 1)
+        square(0, 1, 0)
         t_x(2, 0)
-        m1(1, 0, 1)
+        square(0, 1, 1)
+        t_x(2, 1)
         m1(1, 0, 0)
-        m1(1, 1, 1)
-        copy_x(2, 1, nc.scalar)
-        add(0)
-        square(1, 0, 1)
-        m1(1, 1, 0)
         copy_x(2, 0, nc.vector)
+        copy_x(2, 1, nc.scalar)
+        u_x(3)
+        m1(1, 0, 1)
         square(1, 0, 0)
-        square(1, 1, 1)
-        t_x(3, 1)
-        gain(0)
-        t_x(3, 0)
-        square(1, 1, 0)
-        t_e(0, 1)
-        t_e(0, 0)
+        m1(1, 1, 0)
         q_x(2, 0, 2)
-        m1(2, 0, 1)
+        square(1, 0, 1)
+        t_x(3, 0)
+        add(0)
+        square(1, 1, 0)
+        t_x(3, 1)
+        m1(1, 1, 1)
+        copy_x(3, 0, nc.scalar)
+        u_x(4)
         m1(2, 0, 0)
-        m1(2, 1, 1)
         copy_x(3, 1, nc.scalar)
-        copy_e(0, nc.scalar)
-        add(1)
-        square(2, 0, 1)
-        m1(2, 1, 0)
-        copy_x(3, 0, nc.vector)
-        square(2, 0, 0)
-        square(2, 1, 1)
-        t_x(4, 1)
-        gain(1)
+        gain(0)
+        m1(2, 0, 1)
+        square(1, 1, 1)
         t_x(4, 0)
-        square(2, 1, 0)
-        t_e(1, 1)
-        t_e(1, 0)
-        q_e(0, 0, 2)
+        square(2, 0, 0)
+        t_x(4, 1)
         q_x(3, 0, 2)
-        m1(3, 0, 1)
-        m1(3, 0, 0)
-        m1(3, 1, 1)
-        m2(0, 1)
+        square(2, 0, 1)
+        t_e(0, 0)
+        t_e(0, 1)
+        m1(2, 1, 0)
+        add(1)
+        copy_x(4, 0, nc.scalar)
+        m1(2, 1, 1)
         copy_x(4, 1, nc.scalar)
-        m2(0, 0)
-        copy_e(1, nc.scalar)
-        add(2)
-        square(3, 0, 1)
-        m1(3, 1, 0)
-        copy_x(4, 0, nc.vector)
-        square(3, 0, 0)
-        square(3, 1, 1)
-        t_x(5, 1)
-        copy_o(0, 1, nc.scalar)
-        gain(2)
-        t_x(5, 0)
-        square(3, 1, 0)
-        t_e(2, 1)
-        t_e(2, 0)
-        q_e(1, 0, 2)
+        copy_e(0, nc.vector)
+        m1(3, 0, 0)
+        square(2, 1, 0)
         q_x(4, 0, 2)
-        copy_o(0, 0, nc.vector)
-        m1(4, 0, 1)
-        m1(4, 0, 0)
-        m1(4, 1, 1)
-        m2(1, 1)
+        t_x(5, 0)
+        square(2, 1, 1)
+        q_e(0, 0, 2)
+        t_x(5, 1)
+        square(3, 0, 0)
+        add(2)
+        m1(3, 0, 1)
+        copy_x(5, 0, nc.scalar)
         copy_x(5, 1, nc.scalar)
-        m2(1, 0)
-        copy_e(2, nc.scalar)
-        add(3)
-        square(4, 0, 1)
-        m1(4, 1, 0)
-        copy_x(5, 0, nc.vector)
-        square(4, 0, 0)
-        square(4, 1, 1)
-        t_x(6, 1)
-        copy_o(1, 1, nc.scalar)
-        gain(3)
-        t_x(6, 0)
-        square(4, 1, 0)
-        t_e(3, 1)
-        t_e(3, 0)
-        q_e(2, 0, 2)
+        m1(3, 1, 0)
+        gain(1)
+        square(3, 0, 1)
+        m1(3, 1, 1)
+        square(3, 1, 0)
+        m2(0, 0)
         q_x(5, 0, 2)
-        copy_o(1, 0, nc.vector)
-        m1(5, 0, 1)
-        m1(5, 0, 0)
-        m1(5, 1, 1)
-        m2(2, 1)
+        m2(0, 1)
+        square(3, 1, 1)
+        t_e(1, 0)
+        t_e(1, 1)
+        copy_o(0, 0, nc.vector)
+        t_x(6, 0)
+        copy_o(0, 1, nc.scalar)
+        add(3)
+        t_x(6, 1)
+        copy_e(1, nc.scalar)
+        m1(4, 0, 0)
+        copy_x(6, 0, nc.scalar)
+        q_e(1, 0, 2)
+        m1(4, 0, 1)
         copy_x(6, 1, nc.scalar)
-        m2(2, 0)
-        copy_e(3, nc.scalar)
+        gain(2)
+        m1(4, 1, 0)
+        square(4, 0, 0)
+        m2(1, 0)
+        square(4, 0, 1)
+        q_x(6, 0, 2)
+        m2(1, 1)
+        t_e(2, 0)
+        t_e(2, 1)
+        square(4, 1, 0)
+        copy_o(1, 0, nc.vector)
+        t_x(7, 0)
+        copy_o(1, 1, nc.scalar)
+        copy_e(2, nc.vector)
+        t_x(7, 1)
+        copy_x(7, 0, nc.scalar)
+        gain(3)
+        m1(4, 1, 1)
+        copy_x(7, 1, nc.scalar)
+        m1(5, 0, 0)
+        q_e(2, 0, 2)
+        square(4, 1, 1)
+        m1(5, 0, 1)
+        q_x(7, 0, 2)
+        square(5, 0, 0)
+        t_e(3, 0)
+        t_e(3, 1)
         add(4)
         square(5, 0, 1)
         m1(5, 1, 0)
-        copy_x(6, 0, nc.vector)
-        t_x(7, 1)
-        t_x(7, 0)
-        square(5, 0, 0)
-        square(5, 1, 1)
-        copy_o(2, 1, nc.scalar)
+        copy_e(3, nc.scalar)
+        m1(5, 1, 1)
         gain(4)
         square(5, 1, 0)
-        t_e(4, 1)
-        t_e(4, 0)
-        q_e(3, 0, 2)
-        q_x(6, 0, 2)
-        copy_o(2, 0, nc.vector)
-        m1(6, 0, 1)
+        m2(2, 0)
+        m2(2, 1)
+        square(5, 1, 1)
         m1(6, 0, 0)
-        copy_x(7, 1, nc.scalar)
-        m1(6, 1, 1)
-        m2(3, 1)
-        m2(3, 0)
-        copy_e(4, nc.scalar)
+        q_e(3, 0, 2)
+        copy_o(2, 0, nc.scalar)
+        m1(6, 0, 1)
         add(5)
-        square(6, 0, 1)
-        copy_x(7, 0, nc.vector)
-        m1(6, 1, 0)
         square(6, 0, 0)
-        square(6, 1, 1)
-        copy_o(3, 1, nc.scalar)
+        t_e(4, 0)
+        t_e(4, 1)
+        m1(6, 1, 0)
+        square(6, 0, 1)
+        copy_e(4, nc.vector)
+        copy_o(2, 1, nc.scalar)
+        m1(6, 1, 1)
         gain(5)
-        q_x(7, 0, 2)
         square(6, 1, 0)
-        t_e(5, 1)
-        t_e(5, 0)
-        q_e(4, 0, 2)
-        copy_o(3, 0, nc.vector)
-        m1(7, 1, 0)
-        m2(4, 1)
-        m2(4, 0)
-        copy_e(5, nc.scalar)
-        m1(7, 1, 1)
-        add(6)
-        square(7, 1, 0)
-        copy_o(4, 1, nc.scalar)
-        gain(6)
-        q_e(5, 0, 2)
-        copy_o(4, 0, nc.vector)
-        square_part(7, 1, 1, 0)
-        m1(7, 0, 1)
-        square_part(7, 1, 1, 1)
+        m2(3, 0)
+        m2(3, 1)
+        square(6, 1, 1)
         m1(7, 0, 0)
-        square(7, 0, 1)
-        t_acc(7, 1, 0, 2)
-        t_e(6, 1)
-        t_acc(7, 1, 2, 4)
+        q_e(4, 0, 2)
+        m1(7, 0, 1)
+        copy_o(3, 0, nc.scalar)
+        copy_o(3, 1, nc.vector)
+        t_e(5, 0)
+        t_e(5, 1)
         square(7, 0, 0)
-        t_e(6, 0)
-        copy_e(6, nc.scalar)
-        gain_acc(7, 1)
-        q_e(7, 1, 2)
-        q_e(6, 0, 2)
-        m2(5, 1)
+        add(6)
+        m1(7, 1, 0)
+        square(7, 0, 1)
+        m1(7, 1, 1)
+        copy_e(5, nc.scalar)
+        gain(6)
+        m2(4, 0)
+        square(7, 1, 0)
+        m2(4, 1)
         t_acc(7, 0, 0, 4)
+        square_part(7, 1, 1, 0)
+        q_e(5, 0, 2)
+        copy_o(4, 0, nc.scalar)
+        copy_o(4, 1, nc.vector)
+        t_e(6, 0)
+        t_e(6, 1)
+        square_part(7, 1, 1, 1)
+        t_acc(7, 1, 0, 2)
         gain_acc(7, 0)
-        q_e(7, 0, 1)
         m2(5, 0)
-        copy_o(5, 1, nc.scalar)
-        m2(6, 0)
+        copy_e(6, nc.scalar)
+        m2(5, 1)
+        q_e(7, 0, 1)
+        t_acc(7, 1, 2, 4)
         copy_o(5, 0, nc.scalar)
-        m2_part(7, 1, 1)
-        copy_o(6, 0, nc.vector)
-        m2(7, 0)
-        m2_part(7, 1, 0)
-        copy_o_part(7, 1, 1, nc.scalar)
-        copy_o_part(7, 1, 0, nc.scalar)
+        q_e(6, 0, 2)
+        copy_o(5, 1, nc.vector)
+        m2(6, 0)
+        gain_acc(7, 1)
         m2(6, 1)
-        copy_o(7, 0, nc.vector)
+        copy_o(6, 0, nc.scalar)
+        q_e(7, 1, 2)
         copy_o(6, 1, nc.vector)
+        m2_part(7, 1, 0)
+        m2_part(7, 1, 1)
+        m2(7, 0)
+        copy_o_part(7, 1, 0, nc.scalar)
+        copy_o_part(7, 1, 1, nc.vector)
+        copy_o(7, 0, nc.scalar)

from contextlib import ExitStack

import concourse.mybir as mybir
from concourse.masks import make_identity

G, M, T, A, N = 4, 512, 1024, 512, 512
FLOPS = G * (2 * M * T * 2 * A + 2 * M * A * N)

F32 = mybir.dt.float32
BF16 = mybir.dt.bfloat16
U32 = mybir.dt.uint32
I32 = mybir.dt.int32
U8 = mybir.dt.uint8
FP8X4 = mybir.dt.float8_e4m3fn_x4
FP4X4 = mybir.dt.float4_e2m1fn_x4
ACT = mybir.ActivationFunctionType
ALU = mybir.AluOpType

P = 128
PAIRS = G * M // 256
WARM = 5
RING = {"x": 2, "z": 3, "o": 2, "e": 1}


def tile_cyclostationary_band_detector_s14_kernel(tc, x, basis_words, basis_scales, v, sig_words, sig_scales, out):
    nc = tc.nc
    with ExitStack() as ctx:
        keep = ctx.enter_context(tc.tile_pool(name="keep", bufs=1))
        work = ctx.enter_context(tc.tile_pool(name="work", bufs=5))
        psum = ctx.enter_context(tc.psum_pool(name="psum", bufs=1))
        ctx.enter_context(tc.manual_schedule())

        dummy = keep.tile([P, 16], F32, name="dummy")
        nc.vector.memset(dummy[:], 0.0)
        plane0 = keep.tile([P, 2 * 2 * A], U8, name="plane0", align_bytes=64)
        plane1 = keep.tile([P, 3 * 2 * 2 * A], U8, name="plane1", align_bytes=64)
        splane = keep.tile([P, G * N], U8, name="splane", align_bytes=64)
        vrow = keep.tile([P, G * A], BF16, name="vrow")
        ones = keep.tile([P, P], BF16, name="ones")
        ident = keep.tile([P, P], F32, name="ident")
        warm = keep.tile([P, 512], BF16, name="warm")
        nc.vector.memset(warm[:].bitcast(I32), 0)
        vb = keep.tile([P, G * A], BF16, name="vb")
        vcol = keep.tile([P, 4], BF16, name="vcol")
        nc.vector.memset(vrow[:].bitcast(I32), 0)
        nc.vector.memset(plane0[:].bitcast(I32), 0)
        make_identity(nc, ident[:])
        nc.gpsimd.memset(ones[:], 1.0)
        nc.vector.memset(splane[:].bitcast(I32), 0)
        nc.vector.memset(plane1[:].bitcast(I32), 0)
        nc.scalar.activation(out=dummy[:], in_=dummy[:], func=ACT.Square)

        x_sb = [keep.tile([P, 2, T], BF16, name="x%d" % j) for j in range(PAIRS)]
        bw = [[keep.tile([P, 2, 2 * A], U8, name="bw%d%d" % (b, s), align_bytes=64) for s in range(2)] for b in range(G)]
        sw = keep.tile([P, G, 2 * N], U8, name="sw", align_bytes=64)

        def load_x(j, h):
            r0 = (j % 2) * 256 + h * 128
            nc.sync.dma_start(out=x_sb[j][:, h, :], in_=x[j // 2, r0 : r0 + 128, :])

        def load_x_pair(j):
            r0 = (j % 2) * 256
            nc.sync.dma_start(out=x_sb[j][:], in_=x[j // 2, r0 : r0 + 256, :].rearrange("(h p) k -> p h k", p=P))

        def load_scales(tile, src, r, eng):
            eng.dma_start(
                out=tile[r:P:32, :].bitcast(I32).rearrange("q (g n) -> q g n", g=src.shape[0]),
                in_=src[:, r:16:4, :].bitcast(I32).rearrange("g q n -> q g n"),
            )

        def load_bw(b, s):
            c = slice(2 * A * s, 2 * A * (s + 1))
            nc.sync.dma_start(out=bw[b][s][:], in_=basis_words[2 * b : 2 * b + 2, :, c].rearrange("g p n -> p g n"))

        nc.gpsimd.dma_start(out=vrow[0:1, :], in_=v.rearrange("(o b) a -> o (b a)", o=1))
        for r in range(4):
            load_scales(plane1, basis_scales[2:8], r, nc.gpsimd)
        for r in range(4):
            load_scales(splane, sig_scales, r, nc.gpsimd)
        nc.gpsimd.dma_start(out=vcol[:], in_=v[G - 1].rearrange("(p t) -> p t", t=4))
        load_x(0, 0)
        load_x(0, 1)
        for r in range(4):
            load_scales(plane0, basis_scales[0:2], r, nc.scalar)
        load_x_pair(1)
        load_bw(0, 0)
        load_bw(0, 1)
        load_x_pair(2)
        load_x_pair(3)
        for b in range(1, G):
            load_bw(b, 0)
            load_bw(b, 1)
            if b == 1:
                load_x_pair(4)
                nc.sync.dma_start(out=sw[:], in_=sig_words.rearrange("b p n -> p b n"))
                load_x_pair(5)
            if b == 2:
                load_x_pair(6)
                load_x_pair(7)

        def basis_plane(b):
            return plane0[:] if b == 0 else plane1[:, 2048 * (b - 1) : 2048 * b]

        turn = {"x": 0, "z": 0, "o": 0, "e": 0}

        def ring(kind, dtype=F32, width=512):
            turn[kind] += 1
            return psum.tile([P, width], dtype, name="%s%d" % (kind, turn[kind] % RING[kind]))

        vbank = {}

        xt, xg, xc, xs = {}, {}, {}, {}
        zb, sq, pw, e = {}, {}, {}, {}
        et, eg, ec, es = {}, {}, {}, {}
        ob, osb = {}, {}

        for i in range(WARM):
            wb = psum.tile([P, 512], F32, name="e0")
            nc.tensor.matmul(wb[:], lhsT=warm[:, 0:P], rhs=warm[:], start=True, stop=True)

        def t_x(j, h):
            t = ring("x")
            xt[j, h] = t
            words = x_sb[j][:, h, :].bitcast(F32)
            for g in range(2):
                for u in range(2):
                    c = (2 * g + u) * P
                    if j in xu:
                        nc.tensor.transpose(t[:, c : c + P], xu[j][:, h, c : c + P], ident[:])
                        continue
                    nc.tensor.transpose(t[:, c : c + P], words[:, 256 * g + u : 256 * (g + 1) : 2], ident[:])

        xu = {}

        def u_x(j):
            xu[j] = work.tile([P, 2, 512], F32, name="xu")
            nc.vector.tensor_copy(
                out=xu[j][:].rearrange("p h (g u q) -> p (h g) u q", g=2, u=2),
                in_=x_sb[j][:].rearrange("p h k -> p (h k)").bitcast(F32).rearrange("p (m q u) -> p m u q", m=4, u=2),
            )

        def copy_x(j, h, eng):
            if j not in xg:
                xg[j] = work.tile([P, 2048], BF16, name="xg", align_bytes=64)
            dst = xg[j][:, 1024 * h : 1024 * (h + 1)].bitcast(F32).rearrange("p (g r u) -> p g r u", g=2, u=2)
            src = xt[j, h][:].rearrange("p (g u r) -> p g r u", g=2, u=2)
            if eng is nc.scalar:
                nc.scalar.copy(out=dst, in_=src)
            else:
                nc.vector.tensor_copy(out=dst, in_=src)

        def q_x(j, h0, h1):
            if j not in xc:
                xc[j] = work.tile([P, 512], U32, name="xc", align_bytes=64)
                xs[j] = work.tile([P, 512], U8, name="xs", align_bytes=64)
            nc.vector.quantize_mx(
                out=xc[j][:, 256 * h0 : 256 * h1].bitcast(FP8X4),
                scales=xs[j][:, 256 * h0 : 256 * h1],
                in_=xg[j][:, 1024 * h0 : 1024 * h1],
            )

        def m1(j, h, s):
            b = j // 2
            t = ring("z")
            zb[j, h, s] = t
            for g in range(2):
                c = (2 * h + g) * P
                nc.tensor.matmul_mx(
                    out=t[:],
                    lhsT=xc[j][:, c : c + P].bitcast(FP8X4),
                    lhsT_scale=xs[j][:, c : c + P],
                    rhs=bw[b][s][:, g, :].bitcast(FP4X4),
                    rhs_scale=basis_plane(b)[:, 1024 * g + 512 * s : 1024 * g + 512 * (s + 1)],
                    start=(g == 0),
                    stop=(g == 1),
                )

        def t_x0(h, g):
            t = ring("x")
            xt[0, h, g] = t
            words = x_sb[0][:, h, :].bitcast(F32)
            for u in range(2):
                nc.tensor.transpose(t[:, P * u : P * (u + 1)], words[:, 256 * g + u : 256 * (g + 1) : 2], ident[:])

        def copy_x0(h, g, eng):
            if 0 not in xg:
                xg[0] = work.tile([P, 2048], BF16, name="xg", align_bytes=64)
            c = 512 * (2 * h + g)
            dst = xg[0][:, c : c + 512].bitcast(F32).rearrange("p (r u) -> p r u", u=2)
            src = xt[0, h, g][:, 0:256].rearrange("p (u r) -> p r u", u=2)
            if eng is nc.scalar:
                nc.scalar.copy(out=dst, in_=src)
            else:
                nc.vector.tensor_copy(out=dst, in_=src)

        def q_x0(h, g):
            if 0 not in xc:
                xc[0] = work.tile([P, 512], U32, name="xc", align_bytes=64)
                xs[0] = work.tile([P, 512], U8, name="xs", align_bytes=64)
            c = 2 * h + g
            nc.vector.quantize_mx(
                out=xc[0][:, 128 * c : 128 * (c + 1)].bitcast(FP8X4),
                scales=xs[0][:, 128 * c : 128 * (c + 1)],
                in_=xg[0][:, 512 * c : 512 * (c + 1)],
            )

        def sq_tile(j, h, s):
            if (j, s) not in sq:
                sq[j, s] = work.tile([P, 2, 512], F32, name="sq%d" % s)
            return sq[j, s][:, h, :]

        def square_part(j, h, s, half):
            nc.scalar.activation(
                out=sq_tile(j, h, s)[:, 256 * half : 256 * (half + 1)].rearrange("p (t q) -> p t q", t=2),
                in_=zb[j, h, s][:].rearrange("p (q t) -> p t q", t=4)[:, 2 * half : 2 * half + 2, :],
                func=ACT.Square,
            )

        def square(j, h, s):
            if j == PAIRS - 1:
                nc.scalar.activation(
                    out=sq_tile(j, h, s).rearrange("p (t q) -> p t q", t=4),
                    in_=zb[j, h, s][:].rearrange("p (q t) -> p t q", t=4),
                    func=ACT.Square,
                )
                return
            nc.scalar.activation(
                out=sq_tile(j, h, s).rearrange("p (u q e) -> p u q e", u=2, e=2),
                in_=zb[j, h, s][:].rearrange("p (q u e) -> p u q e", u=2, e=2),
                func=ACT.Square,
            )

        def add(j):
            pw[j] = work.tile([P, 2, 512], F32, name="pw")
            nc.vector.tensor_tensor(out=pw[j][:], in0=sq[j, 0][:], in1=sq[j, 1][:], op=ALU.add)

        def gain(j):
            e[j] = work.tile([P, 2, 512], BF16, name="e")
            b = j // 2
            nc.vector.tensor_tensor(
                out=e[j][:],
                in0=pw[j][:],
                in1=vb[:, 512 * b : 512 * (b + 1)].unsqueeze(1).to_broadcast([P, 2, 512]),
                op=ALU.mult,
            )

        acc = {}

        def t_acc(j, h, t0, t1):
            if t0 == 0:
                acc[j, h] = ring("x")
            for t in range(t0, t1):
                c = slice(P * t, P * (t + 1))
                for s in range(2):
                    nc.tensor.matmul(
                        acc[j, h][:, c], lhsT=sq[j, s][:, h, c], rhs=ident[:], start=(s == 0), stop=(s == 1), is_transpose=True
                    )

        def gain_acc(j, h):
            if j not in eg:
                eg[j] = work.tile([P, 1024], BF16, name="eg", align_bytes=64)
            nc.vector.tensor_tensor(
                out=eg[j][:, 512 * h : 512 * (h + 1)].rearrange("p (r t) -> p r t", t=4),
                in0=acc[j, h][:].rearrange("p (t r) -> p r t", t=4),
                in1=vcol[:].unsqueeze(1).to_broadcast([P, P, 4]),
                op=ALU.mult,
            )

        def v_mm(i):
            t = ring("o", BF16, 1024)
            vbank[i] = t
            for k in range(2):
                c = (2 * i + k) * A
                nc.tensor.matmul(t[:, A * k : A * (k + 1)], lhsT=ones[:], rhs=vrow[:, c : c + A], start=True, stop=True)

        def copy_v(i, eng):
            dst = vb[:, 1024 * i : 1024 * (i + 1)].rearrange("p (b u q e) -> p b u q e", b=2, u=2, e=2)
            src = vbank[i][:].rearrange("p (b q u e) -> p b u q e", b=2, u=2, e=2)
            for k in range(2):
                if eng is nc.scalar:
                    nc.scalar.copy(out=dst[:, k], in_=src[:, k])
                else:
                    nc.vector.tensor_copy(out=dst[:, k], in_=src[:, k])

        def t_e(j, h, u0=0, u1=2):
            if j not in et:
                et[j] = ring("e")
            words = e[j][:, h, :].bitcast(F32)
            for u in range(u0, u1):
                c = (2 * h + u) * P
                nc.tensor.transpose(et[j][:, c : c + P], words[:, P * u : P * (u + 1)], ident[:])

        def copy_e(j, eng):
            eg[j] = work.tile([P, 1024], BF16, name="eg", align_bytes=64)
            dst = eg[j][:].bitcast(F32).rearrange("p (h r u) -> p h r u", h=2, u=2)
            src = et[j][:].rearrange("p (h u r) -> p h r u", h=2, u=2)
            if eng is nc.scalar:
                nc.scalar.copy(out=dst, in_=src)
            else:
                nc.vector.tensor_copy(out=dst, in_=src)

        def q_e(j, h0, h1):
            if j not in ec:
                ec[j] = work.tile([P, 256], U32, name="ec", align_bytes=64)
                es[j] = work.tile([P, 256], U8, name="es", align_bytes=64)
            nc.vector.quantize_mx(
                out=ec[j][:, 128 * h0 : 128 * h1].bitcast(FP8X4),
                scales=es[j][:, 128 * h0 : 128 * h1],
                in_=eg[j][:, 512 * h0 : 512 * h1],
            )

        def m2(j, h):
            b = j // 2
            t = ring("o")
            ob[j, h] = t
            nc.tensor.matmul_mx(
                out=t[:],
                lhsT=ec[j][:, P * h : P * (h + 1)].bitcast(FP8X4),
                lhsT_scale=es[j][:, P * h : P * (h + 1)],
                rhs=sw[:, b, :].bitcast(FP4X4),
                rhs_scale=splane[:, N * b : N * (b + 1)],
                start=True,
                stop=True,
            )

        def m2_part(j, h, n):
            b = j // 2
            t = ring("z")
            ob[j, h, n] = t
            nc.tensor.matmul_mx(
                out=t[:, 0:256],
                lhsT=ec[j][:, P * h : P * (h + 1)].bitcast(FP8X4),
                lhsT_scale=es[j][:, P * h : P * (h + 1)],
                rhs=sw[:, b, 512 * n : 512 * (n + 1)].bitcast(FP4X4),
                rhs_scale=splane[:, N * b + 256 * n : N * b + 256 * (n + 1)],
                start=True,
                stop=True,
            )

        def copy_o_part(j, h, n, eng):
            c = slice(256 * n, 256 * (n + 1))
            if j not in osb:
                osb[j] = work.tile([P, 2, N], F32, name="osb")
            if eng is nc.scalar:
                nc.scalar.copy(out=osb[j][:, h, c], in_=ob[j, h, n][:, 0:256])
            else:
                nc.vector.tensor_copy(out=osb[j][:, h, c], in_=ob[j, h, n][:, 0:256])
            r0 = (j % 2) * 256 + 128 * h
            nc.sync.dma_start(out=out[j // 2, r0 : r0 + 128, c], in_=osb[j][:, h, c])

        def copy_o(j, h, eng):
            if j not in osb:
                osb[j] = work.tile([P, 2, N], F32, name="osb")
            if eng is nc.scalar:
                nc.scalar.copy(out=osb[j][:, h, :], in_=ob[j, h][:])
            else:
                nc.vector.tensor_copy(out=osb[j][:, h, :], in_=ob[j, h][:])
            store(j, h, h + 1)

        def store(j, h0, h1):
            r0 = (j % 2) * 256
            nc.sync.dma_start(
                out=out[j // 2, r0 + 128 * h0 : r0 + 128 * h1, :].rearrange("(h p) n -> p h n", p=P),
                in_=osb[j][:, h0:h1, :],
            )

        t_x(0, 0)
        t_x(0, 1)
        copy_x(0, 0, nc.scalar)
        v_mm(0)
        copy_x(0, 1, nc.scalar)
        v_mm(1)
        u_x(1)
        copy_v(0, nc.scalar)
        q_x(0, 0, 1)
        t_x(1, 0)
        copy_v(1, nc.vector)
        t_x(1, 1)
        m1(0, 0, 0)
        q_x(0, 1, 2)
        copy_x(1, 0, nc.scalar)
        copy_x(1, 1, nc.vector)
        m1(0, 0, 1)
        u_x(2)
        square(0, 0, 0)
        m1(0, 1, 0)
        q_x(1, 0, 2)
        square(0, 0, 1)
        m1(0, 1, 1)
        square(0, 1, 0)
        t_x(2, 0)
        square(0, 1, 1)
        t_x(2, 1)
        m1(1, 0, 0)
        copy_x(2, 0, nc.vector)
        copy_x(2, 1, nc.scalar)
        u_x(3)
        m1(1, 0, 1)
        square(1, 0, 0)
        m1(1, 1, 0)
        q_x(2, 0, 2)
        square(1, 0, 1)
        t_x(3, 0)
        add(0)
        square(1, 1, 0)
        t_x(3, 1)
        m1(1, 1, 1)
        copy_x(3, 0, nc.scalar)
        u_x(4)
        m1(2, 0, 0)
        copy_x(3, 1, nc.scalar)
        gain(0)
        m1(2, 0, 1)
        square(1, 1, 1)
        t_x(4, 0)
        square(2, 0, 0)
        t_x(4, 1)
        q_x(3, 0, 2)
        square(2, 0, 1)
        t_e(0, 0)
        t_e(0, 1)
        m1(2, 1, 0)
        add(1)
        copy_x(4, 0, nc.scalar)
        m1(2, 1, 1)
        copy_x(4, 1, nc.scalar)
        copy_e(0, nc.vector)
        m1(3, 0, 0)
        square(2, 1, 0)
        q_x(4, 0, 2)
        t_x(5, 0)
        square(2, 1, 1)
        q_e(0, 0, 2)
        t_x(5, 1)
        square(3, 0, 0)
        add(2)
        m1(3, 0, 1)
        copy_x(5, 0, nc.scalar)
        copy_x(5, 1, nc.scalar)
        m1(3, 1, 0)
        gain(1)
        square(3, 0, 1)
        m1(3, 1, 1)
        square(3, 1, 0)
        m2(0, 0)
        q_x(5, 0, 2)
        m2(0, 1)
        square(3, 1, 1)
        t_e(1, 0)
        t_e(1, 1)
        copy_o(0, 0, nc.vector)
        t_x(6, 0)
        copy_o(0, 1, nc.scalar)
        add(3)
        t_x(6, 1)
        copy_e(1, nc.scalar)
        m1(4, 0, 0)
        copy_x(6, 0, nc.scalar)
        q_e(1, 0, 2)
        m1(4, 0, 1)
        copy_x(6, 1, nc.scalar)
        gain(2)
        m1(4, 1, 0)
        square(4, 0, 0)
        m2(1, 0)
        square(4, 0, 1)
        q_x(6, 0, 2)
        m2(1, 1)
        t_e(2, 0)
        t_e(2, 1)
        square(4, 1, 0)
        copy_o(1, 0, nc.vector)
        t_x(7, 0)
        copy_o(1, 1, nc.scalar)
        copy_e(2, nc.vector)
        t_x(7, 1)
        copy_x(7, 0, nc.scalar)
        gain(3)
        m1(4, 1, 1)
        copy_x(7, 1, nc.scalar)
        m1(5, 0, 0)
        q_e(2, 0, 2)
        square(4, 1, 1)
        m1(5, 0, 1)
        q_x(7, 0, 2)
        square(5, 0, 0)
        t_e(3, 0)
        t_e(3, 1)
        add(4)
        square(5, 0, 1)
        m1(5, 1, 0)
        copy_e(3, nc.scalar)
        m1(5, 1, 1)
        gain(4)
        square(5, 1, 0)
        m2(2, 0)
        m2(2, 1)
        square(5, 1, 1)
        m1(6, 0, 0)
        q_e(3, 0, 2)
        copy_o(2, 0, nc.scalar)
        m1(6, 0, 1)
        add(5)
        square(6, 0, 0)
        t_e(4, 0)
        t_e(4, 1)
        m1(6, 1, 0)
        square(6, 0, 1)
        copy_e(4, nc.vector)
        copy_o(2, 1, nc.scalar)
        m1(6, 1, 1)
        gain(5)
        square(6, 1, 0)
        m2(3, 0)
        m2(3, 1)
        square(6, 1, 1)
        m1(7, 0, 0)
        q_e(4, 0, 2)
        m1(7, 0, 1)
        copy_o(3, 0, nc.scalar)
        copy_o(3, 1, nc.vector)
        t_e(5, 0)
        t_e(5, 1)
        square(7, 0, 0)
        add(6)
        m1(7, 1, 0)
        square(7, 0, 1)
        m1(7, 1, 1)
        copy_e(5, nc.scalar)
        gain(6)
        m2(4, 0)
        square(7, 1, 0)
        m2(4, 1)
        t_acc(7, 0, 0, 4)
        square_part(7, 1, 1, 0)
        q_e(5, 0, 2)
        copy_o(4, 0, nc.scalar)
        copy_o(4, 1, nc.vector)
        t_e(6, 0)
        t_e(6, 1)
        square_part(7, 1, 1, 1)
        t_acc(7, 1, 0, 2)
        gain_acc(7, 0)
        m2(5, 0)
        copy_e(6, nc.scalar)
        m2(5, 1)
        q_e(7, 0, 1)
        t_acc(7, 1, 2, 4)
        copy_o(5, 0, nc.scalar)
        q_e(6, 0, 2)
        copy_o(5, 1, nc.vector)
        m2(6, 0)
        gain_acc(7, 1)
        m2(6, 1)
        copy_o(6, 0, nc.scalar)
        q_e(7, 1, 2)
        copy_o(6, 1, nc.vector)
        m2_part(7, 1, 0)
        m2_part(7, 1, 1)
        m2(7, 0)
        copy_o_part(7, 1, 0, nc.scalar)
        copy_o_part(7, 1, 1, nc.vector)
        copy_o(7, 0, nc.scalar)
